import numpy as np
import ml_dtypes


def mxq(x, axis, fmt="e4m3"):
    dtype, down = {"e4m3": (ml_dtypes.float8_e4m3fn, 7), "e5m2": (ml_dtypes.float8_e5m2, 14)}[fmt]
    v = np.moveaxis(np.asarray(x, np.float32).astype(ml_dtypes.bfloat16).astype(np.float64), axis, -1)
    blocks = v.reshape(v.shape[:-1] + (-1, 32))
    amax = np.abs(blocks).max(-1, keepdims=True)
    byte = np.maximum(np.where(amax > 0, np.frexp(amax)[1] - 1 + 127, 0) - down, 1)
    scale = np.exp2(byte - 127.0)
    codes = (blocks / scale).astype(np.float32).astype(dtype).astype(np.float64)
    return np.moveaxis((codes * scale).reshape(v.shape), -1, axis)


WIDE = False


def mx_kscale(k):
    if not WIDE:
        return np.ones(k)
    levels = np.array([10, -10, 5, -5, 0])
    if k % 512:
        return np.exp2(np.random.permutation(np.resize(levels, k // 32))).repeat(32)
    a = np.empty((k // 512, 16))
    for p in range(k // 512):
        a[p, :8] = np.random.permutation(np.resize(levels, 8))
        for g in range(8):
            far = levels[np.abs(levels - a[p, g]) >= 10]
            a[p, g + 8] = far[np.random.randint(len(far))]
    return np.exp2(a.ravel()).repeat(32)


def f64(x):
    return np.asarray(x).astype(np.float64)


def striped(idx):
    return np.tile(idx.reshape(-1, 16).T, (8, 1)).astype(np.uint16)


def unstriped(offs):
    return offs[:16].T.reshape(-1).astype(np.int64)


E2M1 = np.array([0.0, 0.5, 1.0, 1.5, 2.0, 3.0, 4.0, 6.0, -0.0, -0.5, -1.0, -1.5, -2.0, -3.0, -4.0, -6.0])


def pack_weight(w, fmt):
    k, n = w.shape
    w = f64(np.asarray(w, np.float32).astype(ml_dtypes.bfloat16)).reshape(k // 32, 32, n)
    amax = np.abs(w).max(1)
    if fmt == "e4m3":
        byte = np.frexp(amax)[1] - 1 + 127 - 7
    else:
        mant, ex = np.frexp(amax / 6.0)
        byte = np.where(mant > 0.5, ex, ex - 1) + 127
    byte = np.clip(np.where(amax > 0, byte, 1), 1, 254)
    scaled = (w * np.exp2(127.0 - byte)[:, None, :]).reshape(k, n).astype(np.float32)
    by_word = np.ascontiguousarray(scaled.reshape(k // 512, 128, 4, n).transpose(0, 1, 3, 2))
    if fmt == "e4m3":
        words = by_word.astype(ml_dtypes.float8_e4m3fn).view(np.uint8)
    else:
        c = by_word.astype(ml_dtypes.float4_e2m1fn).view(np.uint8) & 0xF
        words = (c[..., 0::2] | (c[..., 1::2] << 4)).reshape(k // 512, 128, 2 * n)
    return np.ascontiguousarray(words), np.ascontiguousarray(byte.astype(np.uint8).reshape(k // 512, 16, n))


def unpack_weight(words, scales, fmt):
    g, _, n = scales.shape
    words = np.ascontiguousarray(words).reshape(g, 128, n, -1)
    if fmt == "e4m3":
        vals = words.view(ml_dtypes.float8_e4m3fn).astype(np.float64)
    else:
        nib = np.empty((g, 128, n, 4), np.uint8)
        nib[..., 0::2] = words & 0xF
        nib[..., 1::2] = words >> 4
        vals = E2M1[nib]
    vals = vals * np.repeat(np.exp2(scales.astype(np.float64) - 127.0), 8, axis=1)[..., None]
    return vals.transpose(0, 1, 3, 2).reshape(g * 512, n)


def gelu(v):
    return 0.5 * v * (1.0 + np.tanh(np.sqrt(2.0 / np.pi) * (v + 0.044715 * v**3)))


K, T, S, H, S2, T3, T2, P = 1024, 2048, 512, 1024, 512, 2048, 1024, 512

def setup_inputs():
    n = np.random.standard_normal
    s = mx_kscale(K)[:, None]
    u = mx_kscale(H)[:, None]
    tab_words, tab_scales = pack_weight(n((K, T)) * s, "e4m3")
    tab2_words, tab2_scales = pack_weight(n((H, T3)) / np.sqrt(H) / u, "e4m3")
    w1_words, w1_scales = pack_weight(1.2 * n((K, H)) / np.sqrt(K) / s * u.T, "e2m1")
    return {
        "tab_words": tab_words, "tab_scales": tab_scales,
        "tab2_words": tab2_words, "tab2_scales": tab2_scales,
        "offs": striped(np.random.permutation(T)[:S]),
        "offs2": striped(np.random.permutation(T3)[:S2]),
        "offs3": striped(np.random.permutation(T2)[:S]),
        "pos1": striped(np.random.permutation(T2)[:P]),
        "pos2": striped(np.random.permutation(T2)[:P]),
        "w1_words": w1_words, "w1_scales": w1_scales,
        "w2": (0.58 * n((K, H)) / np.sqrt(K) / s).astype(np.float32),
        "w3": (0.7 * n((K, H)) / np.sqrt(K) / s * u.T).astype(np.float32),
        "page0": (n((H, T2)) * u).astype(np.float32),
        "wgs": np.exp(0.3 * n((128, S))).astype(np.float32),
        "mark": n(S2).astype(np.float32),
        "tie": n((S2, P)).astype(np.float32),
    }

def reference(tab_words, tab_scales, tab2_words, tab2_scales, offs, offs2, offs3, pos1, pos2,
              w1_words, w1_scales, w2, w3, page0, wgs, mark, tie):
    v = unpack_weight(tab_words, tab_scales, "e4m3")[:, unstriped(offs)]
    v2 = unpack_weight(tab2_words, tab2_scales, "e4m3")[:, unstriped(offs2)]
    y1 = unpack_weight(w1_words, w1_scales, "e2m1").T @ v
    y2 = mxq(f64(w2), 0, "e4m3").T @ v
    y3 = mxq(f64(w3), 0, "e4m3").T @ v
    h = y1 * np.cos(y2) + y3
    page = f64(page0).copy()
    page[:, unstriped(offs3)] = np.tile(f64(wgs), (H // 128, 1)) * h
    e = v2.T @ mxq(page, 0, "e4m3")
    first = e[:, unstriped(pos1)]
    second = e[:, unstriped(pos2)]
    return first * f64(mark)[:, None] + second * f64(tie)

@@ -1,0 +1,297 @@
+from contextlib import ExitStack
+
+import concourse.mybir as mybir
+
+F32 = mybir.dt.float32
+BF16 = mybir.dt.bfloat16
+I32 = mybir.dt.int32
+U32 = mybir.dt.uint32
+U16 = mybir.dt.uint16
+U8 = mybir.dt.uint8
+FP8X4 = mybir.dt.float8_e4m3fn_x4
+FP4X4 = mybir.dt.float4_e2m1fn_x4
+ALU = mybir.AluOpType
+ACT = mybir.ActivationFunctionType
+
+P = 128
+PACK = 4
+PASS = P * PACK
+K, T, S, H, S2, T3, T2, PAIRS = 1024, 2048, 512, 1024, 512, 2048, 1024, 512
+PASSES = 2
+SLICES = H // P
+HALF = 512
+FLOPS = 2 * (3 * K * H * S + H * S2 * T2)
+
+
+def tile_list_welllog_marker_matcher_kernel(
+    tc, tab_words, tab_scales, tab2_words, tab2_scales, offs, offs2, offs3, pos1, pos2,
+    w1_words, w1_scales, w2, w3, page0, wgs, mark, tie, out,
+):
+    nc = tc.nc
+    with ExitStack() as ctx:
+        lists = ctx.enter_context(tc.tile_pool(name="lists", bufs=1))
+        keep = ctx.enter_context(tc.tile_pool(name="keep", bufs=1))
+        psum = ctx.enter_context(tc.psum_pool(name="psum", bufs=1))
+
+        def sb(name, shape, dtype):
+            return keep.tile(shape, dtype, name=name, tag=name, align_bytes=64)
+
+        def many(name, count, shape, dtype):
+            return [sb("%s%d" % (name, i), shape, dtype) for i in range(count)]
+
+        def load_list(name, src):
+            tile = lists.tile([P, 32], U16, name=name)
+            nc.sync.dma_start(tile[:], src)
+            return tile
+
+        banks = [psum.tile([P, HALF], F32, name="bank%d" % i) for i in range(8)]
+
+        tab_w = many("tab_w", PASSES, [P, T], U32)
+        tab_s = sb("tab_s", [P, PASSES, T], U8)
+        tab2_w = many("tab2_w", PASSES, [P, T3], U32)
+        tab2_s = sb("tab2_s", [P, T3], U8)
+        v_w = many("v_w", PASSES, [P, S], U32)
+        v_s = many("v_s", PASSES, [P, S], U8)
+        v2_w = many("v2_w", 1, [P, PASSES, S2 // 2], U32)
+        v2_s = many("v2_s", 1, [P, S2 // 2], U8)
+        w1_w = sb("w1_w", [P, PASSES * H], U16)
+        w1_s = sb("w1_s", [P, PASSES, H], U8)
+        w1_wd = sb("w1_wd", [P, PASSES * H], U16)
+        w1_sd = sb("w1_sd", [P, PASSES * H], U8)
+        raw = many("raw", 4, [P, PACK, HALF], F32)
+        rounded = many("rounded", 3, [P, PACK * HALF], BF16)
+        w_c = many("w_c", 8, [P, HALF], U32)
+        w_s = many("w_s", 8, [P, HALF], U8)
+        page = many("page", SLICES, [P, T2], F32)
+        page_c = many("page_c", 4, [P, HALF], U32)
+        page_s = many("page_s", 4, [P, HALF], U8)
+        feat = many("feat", SLICES, [P, S], F32)
+        gain = many("gain", 2, [P, 2, S], F32)
+        score = many("score", 4, [P, T2], F32)
+        tie_t = sb("tie_t", [P, 4, PAIRS], F32)
+        mark_t = sb("mark_t", [P, 4], F32)
+        first = many("first", 4, [P, PAIRS], F32)
+        second = many("second", 2, [P, PAIRS], F32)
+
+        def load_words(tile, words):
+            nc.sync.dma_start(tile[:].bitcast(I32), words.rearrange("p t i -> p (t i)").bitcast(I32))
+
+        def load_chunk(n):
+            b, a = n // 4, n % 2
+            w = w2 if n % 4 < 2 else w3
+            src = w[PASS * a : PASS * (a + 1), PASS * b : PASS * (b + 1)]
+            nc.sync.dma_start(raw[n % 4][:], src.rearrange("(p j) c -> p j c", j=PACK))
+
+        def copy_on(engine, dst, src):
+            if engine == "scalar":
+                nc.scalar.copy(dst, src)
+            else:
+                nc.vector.tensor_copy(dst, src)
+
+        def quantise_chunk(n, engine, t0=0, t1=PACK):
+            dst = rounded[n % 3]
+            copy_on(
+                engine,
+                dst[:].rearrange("p (t m j) -> p m j t", t=PACK, j=PACK)[:, :, :, t0:t1],
+                raw[n % 4][:].rearrange("p j (m t) -> p m j t", t=PACK)[:, :, :, t0:t1],
+            )
+            nc.vector.quantize_mx(
+                out=w_c[n][:, P * t0 : P * t1].bitcast(FP8X4),
+                scales=w_s[n][:, P * t0 : P * t1],
+                in_=dst[:, PASS * t0 : PASS * t1],
+            )
+
+        page_rows = page0.rearrange("(b p t) n -> b t p n", p=P, t=PACK)
+
+        def load_page(s):
+            nc.sync.dma_start(page[s][:], page_rows[s // PACK, s % PACK])
+
+        gain_rows = wgs.rearrange("(q t) j -> q t j", t=PACK)
+
+        def load_gain(u):
+            for quad in range(4):
+                nc.sync.dma_start(gain[u][32 * quad : 32 * quad + 32], gain_rows[:, 2 * u : 2 * u + 2, :])
+
+        nc.vector.memset(tab_s[:].rearrange("p a t -> p (a t)").bitcast(I32), 0)
+        nc.vector.memset(w1_s[:].rearrange("p a t -> p (a t)").bitcast(I32), 0)
+        nc.vector.memset(tab2_s[:].bitcast(I32), 0)
+        idx = load_list("idx", offs)
+        for a in range(PASSES):
+            load_words(tab_w[a], tab_words[a])
+            load_chunk(a)
+        nc.sync.dma_start(
+            w1_w[:].bitcast(I32).rearrange("p (a c) -> p a c", a=PASSES),
+            w1_words.rearrange("a p c -> p a c").bitcast(I32),
+        )
+        for src, dst in ((tab_scales, tab_s), (w1_scales, w1_s)):
+            for r in range(4):
+                nc.gpsimd.dma_start(
+                    dst[r:P:32].bitcast(I32),
+                    src[:, r:16:4, :].rearrange("a q t -> q a t").bitcast(I32),
+                )
+        for n in (2, 3):
+            load_chunk(n)
+        idx3 = load_list("idx3", offs3)
+        load_page(0)
+        load_gain(0)
+
+        for a in range(PASSES):
+            nc.vector.tensor_copy(v_w[a][:], tab_w[a][:].indirect(idx[:]))
+            nc.vector.tensor_copy(v_s[a][:], tab_s[:, a, :].indirect(idx[:]))
+        nc.vector.tensor_copy(
+            w1_wd[:].rearrange("p (g t m) -> p g m t", t=PACK, m=P),
+            w1_w[:].rearrange("p (g m t) -> p g m t", t=PACK, m=P),
+        )
+        nc.vector.tensor_copy(
+            w1_sd[:].rearrange("p (g t m) -> p g m t", t=PACK, m=P),
+            w1_s[:].rearrange("p a (b m t) -> p (a b) m t", t=PACK, m=P),
+        )
+        for n in range(3):
+            quantise_chunk(n, "scalar" if n < 2 else "vector")
+        quantise_chunk(3, "vector", 0, 1)
+
+        def later_loads():
+            load_chunk(4)
+            load_page(1)
+            load_chunk(5)
+            load_gain(1)
+            load_page(2)
+            load_chunk(6)
+            load_chunk(7)
+            for s in (3, 4, 5):
+                load_page(s)
+            idx2 = load_list("idx2", offs2)
+            for a in range(PASSES):
+                load_words(tab2_w[a], tab2_words[a])
+            for quad in range(4):
+                nc.sync.dma_start(
+                    tab2_s[32 * quad : 32 * quad + 8, :].bitcast(I32),
+                    tab2_scales[:, 4 * quad : 4 * quad + 4, :].bitcast(I32),
+                )
+            load_page(6)
+            load_page(7)
+            nc.sync.dma_start(tie_t[:], tie.rearrange("(c p) j -> p c j", p=P))
+            p1 = load_list("p1", pos1)
+            p2 = load_list("p2", pos2)
+            with nc.allow_non_contiguous_dma("one value of mark for each partition and row tile"):
+                nc.sync.dma_start(mark_t[:], mark.rearrange("(c p) -> p c", p=P))
+            return idx2, p1, p2
+
+        def product(bank, s, which):
+            b, t = s // PACK, s % PACK
+            for a in range(PASSES):
+                if which == 1:
+                    cols = slice(H * a + P * s, H * a + P * (s + 1))
+                    lhs, lhs_s = w1_wd[:, cols].bitcast(FP4X4), w1_sd[:, cols]
+                else:
+                    n = 4 * b + 2 * (which - 2) + a
+                    cols = slice(P * t, P * (t + 1))
+                    lhs, lhs_s = w_c[n][:, cols].bitcast(FP8X4), w_s[n][:, cols]
+                nc.tensor.matmul_mx(
+                    out=bank[:], lhsT=lhs, lhsT_scale=lhs_s, rhs=v_w[a][:].bitcast(FP8X4), rhs_scale=v_s[a][:],
+                    start=(a == 0), stop=(a == PASSES - 1),
+                )
+
+        def front(s):
+            y2, y1 = banks[s % 2], banks[2 + s % 3]
+            product(y2, s, 2)
+            nc.scalar.activation(feat[s][:], y2[:], ACT.Sin, scale=0.5)
+            nc.scalar.activation(feat[s][:], feat[s][:], ACT.Square)
+            product(y1, s, 1)
+            nc.vector.scalar_tensor_tensor(feat[s][:], feat[s][:], 0.5, y1[:], ALU.subtract, ALU.mult)
+
+        def middle(s):
+            y3 = banks[5 + s % 3]
+            product(y3, s, 3)
+            nc.vector.scalar_tensor_tensor(feat[s][:], feat[s][:], -2.0, y3[:], ALU.mult, ALU.add)
+
+        def place(s):
+            t = s % PACK
+            nc.vector.tensor_tensor(page[s][:].indirect(idx3[:]), feat[s][:], gain[t // 2][:, t % 2, :], ALU.mult)
+
+        def staging(b, h):
+            return raw[2 * (1 - b) + h]
+
+        def stage(s):
+            for h in range(2):
+                nc.sync.dma_start(staging(s // PACK, h)[:, s % PACK, :], page[s][:, HALF * h : HALF * (h + 1)])
+
+        def round_page(b, h, engine, n0, n1):
+            dst = rounded[(8 + 2 * b + h) % 3]
+            copy_on(
+                engine,
+                dst[:, PACK * n0 : PACK * n1].rearrange("p (c i t) -> p c t i", t=PACK, i=4),
+                staging(b, h)[:, :, n0:n1].rearrange("p t (c i) -> p c t i", i=4),
+            )
+
+        def quantise_page(b, h):
+            n = 2 * b + h
+            nc.vector.quantize_mx(out=page_c[n][:].bitcast(FP8X4), scales=page_s[n][:], in_=rounded[(8 + n) % 3][:])
+
+        def gather_candidates(words, scales, half):
+            part = idx2[:, 16 * half : 16 * (half + 1)]
+            for a in range(PASSES):
+                nc.vector.tensor_copy(words[:, a, :], tab2_w[a][:].indirect(part))
+            nc.vector.tensor_copy(scales[:], tab2_s[:].indirect(part))
+
+        front(0)
+        middle(0)
+        for s in range(SLICES):
+            if s == 3:
+                for n in range(4, 8):
+                    quantise_chunk(n, "scalar")
+            if s + 1 < SLICES:
+                front(s + 1)
+            if s == 0:
+                quantise_chunk(3, "scalar", 1, PACK)
+                idx2, p1, p2 = later_loads()
+            place(s)
+            if s + 1 < SLICES:
+                middle(s + 1)
+            if s == PACK - 1:
+                for t in range(PACK):
+                    stage(t)
+            elif PACK <= s < SLICES - 1:
+                stage(s)
+            if s == SLICES - 2:
+                gather_candidates(v2_w[0], v2_s[0], 0)
+                for h in range(2):
+                    round_page(0, h, "scalar", 0, HALF)
+                    quantise_page(0, h)
+
+        last = SLICES - 1
+        for h in (1, 0):
+            nc.vector.tensor_copy(staging(1, h)[:, PACK - 1, :], page[last][:, HALF * h : HALF * (h + 1)])
+        round_page(1, 1, "scalar", HALF // 2, HALF)
+        round_page(1, 0, "vector", 0, HALF)
+        round_page(1, 1, "vector", 0, HALF // 2)
+        for h in range(2):
+            quantise_page(1, h)
+        v2_w.append(keep.tile([P, PASSES, S2 // 2], U32, name="v2_w1", tag="rounded2", align_bytes=64))
+        v2_s.append(keep.tile([P, S2 // 2], U8, name="v2_s1", tag="rounded1", align_bytes=64))
+        gather_candidates(v2_w[1], v2_s[1], 1)
+
+        score_banks = ((4, 7), (0, 1), (2, 5), (3, 6))
+
+        def combine(m):
+            nc.vector.scalar_tensor_tensor(
+                first[m][:], first[m][:], mark_t[:, m : m + 1], second[m % 2][:], ALU.mult, ALU.add
+            )
+            nc.sync.dma_start(out[P * m : P * (m + 1), :], first[m][:])
+
+        for m in range(4):
+            cols = slice(P * (m % 2), P * (m % 2 + 1))
+            for h in range(2):
+                bank = banks[score_banks[m][h]]
+                for a in range(PASSES):
+                    nc.tensor.matmul_mx(
+                        out=bank[:], lhsT=v2_w[m // 2][:, a, cols].bitcast(FP8X4), lhsT_scale=v2_s[m // 2][4 * a : P, cols],
+                        rhs=page_c[2 * a + h][:].bitcast(FP8X4), rhs_scale=page_s[2 * a + h][:],
+                        start=(a == 0), stop=(a == PASSES - 1),
+                    )
+                nc.scalar.copy(score[m][:, HALF * h : HALF * (h + 1)], bank[:])
+            nc.vector.tensor_tensor(second[m % 2][:], score[m][:].indirect(p2[:]), tie_t[:, m, :], ALU.mult)
+            if m > 0:
+                combine(m - 1)
+            nc.vector.tensor_copy(first[m][:], score[m][:].indirect(p1[:]))
+        combine(3)

@@ -52,8 +52,7 @@ def tile_list_welllog_marker_matcher_kernel(
         tab2_s = sb("tab2_s", [P, T3], U8)
         v_w = many("v_w", PASSES, [P, S], U32)
         v_s = many("v_s", PASSES, [P, S], U8)
-        v2_w = many("v2_w", 1, [P, PASSES, S2 // 2], U32)
-        v2_s = many("v2_s", 1, [P, S2 // 2], U8)
+        v2_w = []
         w1_w = sb("w1_w", [P, PASSES * H], U16)
         w1_s = sb("w1_s", [P, PASSES, H], U8)
         w1_wd = sb("w1_wd", [P, PASSES * H], U16)
@@ -65,8 +64,8 @@ def tile_list_welllog_marker_matcher_kernel(
         page = many("page", SLICES, [P, T2], F32)
         page_c = many("page_c", 4, [P, HALF], U32)
         page_s = many("page_s", 4, [P, HALF], U8)
-        feat = many("feat", SLICES, [P, S], F32)
-        gain = many("gain", 2, [P, 2, S], F32)
+        feat = [tile[:] for tile in many("feat", PACK, [P, S], F32)]
+        gain = many("gain", PACK, [P, S], F32)
         score = many("score", 4, [P, T2], F32)
         tie_t = sb("tie_t", [P, 4, PAIRS], F32)
         mark_t = sb("mark_t", [P, 4], F32)
@@ -108,32 +107,36 @@ def tile_list_welllog_marker_matcher_kernel(
 
         gain_rows = wgs.rearrange("(q t) j -> q t j", t=PACK)
 
-        def load_gain(u):
+        def load_gain(t):
             for quad in range(4):
-                nc.sync.dma_start(gain[u][32 * quad : 32 * quad + 32], gain_rows[:, 2 * u : 2 * u + 2, :])
+                nc.sync.dma_start(gain[t][32 * quad : 32 * quad + 32, :], gain_rows[:, t, :])
 
         nc.vector.memset(tab_s[:].rearrange("p a t -> p (a t)").bitcast(I32), 0)
         nc.vector.memset(w1_s[:].rearrange("p a t -> p (a t)").bitcast(I32), 0)
         nc.vector.memset(tab2_s[:].bitcast(I32), 0)
+        def load_scale_rows(dst, src):
+            for r in range(4):
+                nc.sync.dma_start(
+                    dst[r:P:32].bitcast(I32),
+                    src[:, r:16:4, :].rearrange("a q t -> q a t").bitcast(I32),
+                )
+
         idx = load_list("idx", offs)
-        for a in range(PASSES):
-            load_words(tab_w[a], tab_words[a])
-            load_chunk(a)
+        load_words(tab_w[0], tab_words[0])
+        load_scale_rows(tab_s, tab_scales)
         nc.sync.dma_start(
             w1_w[:].bitcast(I32).rearrange("p (a c) -> p a c", a=PASSES),
             w1_words.rearrange("a p c -> p a c").bitcast(I32),
         )
-        for src, dst in ((tab_scales, tab_s), (w1_scales, w1_s)):
-            for r in range(4):
-                nc.gpsimd.dma_start(
-                    dst[r:P:32].bitcast(I32),
-                    src[:, r:16:4, :].rearrange("a q t -> q a t").bitcast(I32),
-                )
-        for n in (2, 3):
-            load_chunk(n)
+        load_chunk(0)
+        load_scale_rows(w1_s, w1_scales)
+        load_chunk(1)
+        load_words(tab_w[1], tab_words[1])
+        load_chunk(2)
         idx3 = load_list("idx3", offs3)
-        load_page(0)
         load_gain(0)
+        load_chunk(3)
+        load_page(0)
 
         for a in range(PASSES):
             nc.vector.tensor_copy(v_w[a][:], tab_w[a][:].indirect(idx[:]))
@@ -150,16 +153,22 @@ def tile_list_welllog_marker_matcher_kernel(
             quantise_chunk(n, "scalar" if n < 2 else "vector")
         quantise_chunk(3, "vector", 0, 1)
 
-        def later_loads():
-            load_chunk(4)
+        def second_loads():
             load_page(1)
-            load_chunk(5)
             load_gain(1)
+            load_chunk(4)
+            load_gain(2)
             load_page(2)
+            load_chunk(5)
             load_chunk(6)
+            load_gain(3)
             load_chunk(7)
-            for s in (3, 4, 5):
-                load_page(s)
+            load_page(3)
+            load_page(4)
+
+        def third_loads():
+            load_page(5)
+            load_page(6)
             idx2 = load_list("idx2", offs2)
             for a in range(PASSES):
                 load_words(tab2_w[a], tab2_words[a])
@@ -168,7 +177,6 @@ def tile_list_welllog_marker_matcher_kernel(
                     tab2_s[32 * quad : 32 * quad + 8, :].bitcast(I32),
                     tab2_scales[:, 4 * quad : 4 * quad + 4, :].bitcast(I32),
                 )
-            load_page(6)
             load_page(7)
             nc.sync.dma_start(tie_t[:], tie.rearrange("(c p) j -> p c j", p=P))
             p1 = load_list("p1", pos1)
@@ -192,84 +200,88 @@ def tile_list_welllog_marker_matcher_kernel(
                     start=(a == 0), stop=(a == PASSES - 1),
                 )
 
-        def front(s):
-            y2, y1 = banks[s % 2], banks[2 + s % 3]
+        def angle(s):
+            y2 = banks[5 if s in (1, 2, 3) else s % 2]
             product(y2, s, 2)
-            nc.scalar.activation(feat[s][:], y2[:], ACT.Sin, scale=0.5)
-            nc.scalar.activation(feat[s][:], feat[s][:], ACT.Square)
+            nc.scalar.activation(feat[s], y2[:], ACT.Sin, scale=0.5)
+            nc.scalar.activation(feat[s], feat[s], ACT.Square)
+
+        def front(s):
+            y1 = banks[2 + s % 3]
             product(y1, s, 1)
-            nc.vector.scalar_tensor_tensor(feat[s][:], feat[s][:], 0.5, y1[:], ALU.subtract, ALU.mult)
+            nc.vector.scalar_tensor_tensor(feat[s], feat[s], 0.5, y1[:], ALU.subtract, ALU.mult)
 
         def middle(s):
             y3 = banks[5 + s % 3]
             product(y3, s, 3)
-            nc.vector.scalar_tensor_tensor(feat[s][:], feat[s][:], -2.0, y3[:], ALU.mult, ALU.add)
+            nc.vector.scalar_tensor_tensor(feat[s], feat[s], -2.0, y3[:], ALU.mult, ALU.add)
 
         def place(s):
-            t = s % PACK
-            nc.vector.tensor_tensor(page[s][:].indirect(idx3[:]), feat[s][:], gain[t // 2][:, t % 2, :], ALU.mult)
+            nc.vector.tensor_tensor(page[s][:].indirect(idx3[:]), feat[s], gain[s % PACK][:], ALU.mult)
 
-        def staging(b, h):
-            return raw[2 * (1 - b) + h]
+        def reuse(name, tag, shape, dtype):
+            return keep.tile(shape, dtype, name=name, tag=tag, align_bytes=64)
 
-        def stage(s):
+        def stage(t):
             for h in range(2):
-                nc.sync.dma_start(staging(s // PACK, h)[:, s % PACK, :], page[s][:, HALF * h : HALF * (h + 1)])
+                nc.sync.dma_start(raw[h][:, t, :], page[t][:, HALF * h : HALF * (h + 1)])
 
-        def round_page(b, h, engine, n0, n1):
-            dst = rounded[(8 + 2 * b + h) % 3]
-            copy_on(
-                engine,
-                dst[:, PACK * n0 : PACK * n1].rearrange("p (c i t) -> p c t i", t=PACK, i=4),
-                staging(b, h)[:, :, n0:n1].rearrange("p t (c i) -> p c t i", i=4),
-            )
+        def quantise_page(n, src):
+            nc.vector.quantize_mx(out=page_c[n][:].bitcast(FP8X4), scales=page_s[n][:], in_=src[:])
 
-        def quantise_page(b, h):
-            n = 2 * b + h
-            nc.vector.quantize_mx(out=page_c[n][:].bitcast(FP8X4), scales=page_s[n][:], in_=rounded[(8 + n) % 3][:])
-
-        def gather_candidates(words, scales, half):
-            part = idx2[:, 16 * half : 16 * (half + 1)]
+        def gather_candidates(half, tag):
+            words = reuse("v2_w%d" % half, tag, [P, PASSES, S2 // 2], U32)
             for a in range(PASSES):
-                nc.vector.tensor_copy(words[:, a, :], tab2_w[a][:].indirect(part))
-            nc.vector.tensor_copy(scales[:], tab2_s[:].indirect(part))
+                nc.vector.tensor_copy(words[:, a, :], tab2_w[a][:].indirect(idx2[:, 16 * half : 16 * (half + 1)]))
+            v2_w.append(words)
 
+        woven = []
+        angle(0)
         front(0)
         middle(0)
+        quantise_chunk(3, "scalar", 1, PACK)
+        for s in range(1, PACK):
+            angle(s)
+        second_loads()
         for s in range(SLICES):
             if s == 3:
                 for n in range(4, 8):
                     quantise_chunk(n, "scalar")
+                feat_late = reuse("feat_late", "raw3", [P, PACK, S], F32)
+                feat.extend([feat_late[:, t, :] for t in range(PACK)])
+                for later in range(PACK, SLICES):
+                    angle(later)
             if s + 1 < SLICES:
                 front(s + 1)
-            if s == 0:
-                quantise_chunk(3, "scalar", 1, PACK)
-                idx2, p1, p2 = later_loads()
             place(s)
             if s + 1 < SLICES:
                 middle(s + 1)
             if s == PACK - 1:
                 for t in range(PACK):
                     stage(t)
-            elif PACK <= s < SLICES - 1:
-                stage(s)
-            if s == SLICES - 2:
-                gather_candidates(v2_w[0], v2_s[0], 0)
+                idx2, p1, p2 = third_loads()
                 for h in range(2):
-                    round_page(0, h, "scalar", 0, HALF)
-                    quantise_page(0, h)
+                    dst = rounded[(8 + h) % 3]
+                    nc.scalar.copy(
+                        dst[:].rearrange("p (c i t) -> p c t i", t=PACK, i=4),
+                        raw[h][:].rearrange("p t (c i) -> p c t i", i=4),
+                    )
+                    quantise_page(h, dst)
+                    woven.append(reuse("woven%d" % h, "raw%d" % h, [P, PACK * HALF], BF16))
+            if s == SLICES - 1:
+                v2_s = reuse("v2_s", "gain3", [P, S2], U8)
+                nc.vector.tensor_copy(v2_s[:], tab2_s[:].indirect(idx2[:]))
+                gather_candidates(0, "raw3")
+            if s >= PACK:
+                for h in range(2):
+                    nc.scalar.copy(
+                        woven[h][:].rearrange("p (n t) -> p n t", t=PACK)[:, :, s - PACK],
+                        page[s][:, HALF * h : HALF * (h + 1)],
+                    )
 
-        last = SLICES - 1
-        for h in (1, 0):
-            nc.vector.tensor_copy(staging(1, h)[:, PACK - 1, :], page[last][:, HALF * h : HALF * (h + 1)])
-        round_page(1, 1, "scalar", HALF // 2, HALF)
-        round_page(1, 0, "vector", 0, HALF)
-        round_page(1, 1, "vector", 0, HALF // 2)
         for h in range(2):
-            quantise_page(1, h)
-        v2_w.append(keep.tile([P, PASSES, S2 // 2], U32, name="v2_w1", tag="rounded2", align_bytes=64))
-        v2_s.append(keep.tile([P, S2 // 2], U8, name="v2_s1", tag="rounded1", align_bytes=64))
-        gather_candidates(v2_w[1], v2_s[1], 1)
+            quantise_page(2 + h, woven[h])
+        gather_candidates(1, "raw1")
 
         score_banks = ((4, 7), (0, 1), (2, 5), (3, 6))
 
@@ -285,7 +297,7 @@ def tile_list_welllog_marker_matcher_kernel(
                 bank = banks[score_banks[m][h]]
                 for a in range(PASSES):
                     nc.tensor.matmul_mx(
-                        out=bank[:], lhsT=v2_w[m // 2][:, a, cols].bitcast(FP8X4), lhsT_scale=v2_s[m // 2][4 * a : P, cols],
+                        out=bank[:], lhsT=v2_w[m // 2][:, a, cols].bitcast(FP8X4), lhsT_scale=v2_s[4 * a : P, P * m : P * (m + 1)],
                         rhs=page_c[2 * a + h][:].bitcast(FP8X4), rhs_scale=page_s[2 * a + h][:],
                         start=(a == 0), stop=(a == PASSES - 1),
                     )

@@ -1,6 +1,7 @@
 from contextlib import ExitStack
 
 import concourse.mybir as mybir
+from concourse.masks import make_identity
 
 F32 = mybir.dt.float32
 BF16 = mybir.dt.bfloat16
@@ -36,6 +37,9 @@ def tile_list_welllog_marker_matcher_kernel(
         def sb(name, shape, dtype):
             return keep.tile(shape, dtype, name=name, tag=name, align_bytes=64)
 
+        def reuse(name, tag, shape, dtype):
+            return keep.tile(shape, dtype, name=name, tag=tag, align_bytes=64)
+
         def many(name, count, shape, dtype):
             return [sb("%s%d" % (name, i), shape, dtype) for i in range(count)]
 
@@ -55,17 +59,18 @@ def tile_list_welllog_marker_matcher_kernel(
         v2_w = []
         w1_w = sb("w1_w", [P, PASSES * H], U16)
         w1_s = sb("w1_s", [P, PASSES, H], U8)
-        w1_wd = sb("w1_wd", [P, PASSES * H], U16)
-        w1_sd = sb("w1_sd", [P, PASSES * H], U8)
         raw = many("raw", 4, [P, PACK, HALF], F32)
-        rounded = many("rounded", 3, [P, PACK * HALF], BF16)
         w_c = many("w_c", 8, [P, HALF], U32)
         w_s = many("w_s", 8, [P, HALF], U8)
         page = many("page", SLICES, [P, T2], F32)
         page_c = many("page_c", 4, [P, HALF], U32)
         page_s = many("page_s", 4, [P, HALF], U8)
-        feat = [tile[:] for tile in many("feat", PACK, [P, S], F32)]
+        feat = many("feat", 4, [P, PASS], F32)
+        turned = [tile[:] for tile in many("turned", 2, [P, S], F32)]
         gain = many("gain", PACK, [P, S], F32)
+        ident = sb("ident", [P, P], F32)
+        wgs_t = reuse("wgs_t", "early", [P, S], F32)
+        wgs_turned = reuse("wgs_turned", "late", [P, 4, PACK * P], F32)
         score = many("score", 4, [P, T2], F32)
         tie_t = sb("tie_t", [P, 4, PAIRS], F32)
         mark_t = sb("mark_t", [P, 4], F32)
@@ -87,29 +92,39 @@ def tile_list_welllog_marker_matcher_kernel(
             else:
                 nc.vector.tensor_copy(dst, src)
 
-        def quantise_chunk(n, engine, t0=0, t1=PACK):
-            dst = rounded[n % 3]
+        def weave(engine, dst, src):
             copy_on(
                 engine,
-                dst[:].rearrange("p (t m j) -> p m j t", t=PACK, j=PACK)[:, :, :, t0:t1],
-                raw[n % 4][:].rearrange("p j (m t) -> p m j t", t=PACK)[:, :, :, t0:t1],
+                dst.rearrange("p (c i t) -> p c t i", t=PACK, i=2),
+                src.rearrange("p t (c i) -> p c t i", i=2),
             )
-            nc.vector.quantize_mx(
-                out=w_c[n][:, P * t0 : P * t1].bitcast(FP8X4),
-                scales=w_s[n][:, P * t0 : P * t1],
-                in_=dst[:, PASS * t0 : PASS * t1],
-            )
+
+        def rounded(n):
+            return reuse("rounded%d" % n, "rounded_slot%d" % (n % 3), [P, PACK * HALF], BF16)[:]
+
+        def quantise_chunk(n, dst, engine):
+            weave(engine, dst, raw[n % 4][:])
+            nc.vector.quantize_mx(out=w_c[n][:].bitcast(FP8X4), scales=w_s[n][:], in_=dst)
 
         page_rows = page0.rearrange("(b p t) n -> b t p n", p=P, t=PACK)
 
         def load_page(s):
             nc.sync.dma_start(page[s][:], page_rows[s // PACK, s % PACK])
 
-        gain_rows = wgs.rearrange("(q t) j -> q t j", t=PACK)
-
-        def load_gain(t):
-            for quad in range(4):
-                nc.sync.dma_start(gain[t][32 * quad : 32 * quad + 32, :], gain_rows[:, t, :])
+        def deal_gain():
+            for c in range(4):
+                nc.tensor.transpose(banks[7][:, P * c : P * (c + 1)], wgs_t[:, P * c : P * (c + 1)], ident[:])
+            rows = banks[7][:].rearrange("p (c q t) -> p t c q", c=4, t=PACK)
+            for t in range(PACK):
+                nc.scalar.copy(
+                    wgs_turned[:, t, :].rearrange("p (c g q) -> p c g q", c=4, g=4),
+                    rows[:, t].unsqueeze(2).to_broadcast([P, 4, 4, 32]),
+                )
+            for t in range(PACK):
+                bank = banks[(6, 4, 1, 7)[t]]
+                for c in range(4):
+                    nc.tensor.transpose(bank[:, P * c : P * (c + 1)], wgs_turned[:, t, P * c : P * (c + 1)], ident[:])
+                nc.scalar.copy(gain[t][:], bank[:])
 
         nc.vector.memset(tab_s[:].rearrange("p a t -> p (a t)").bitcast(I32), 0)
         nc.vector.memset(w1_s[:].rearrange("p a t -> p (a t)").bitcast(I32), 0)
@@ -121,7 +136,9 @@ def tile_list_welllog_marker_matcher_kernel(
                     src[:, r:16:4, :].rearrange("a q t -> q a t").bitcast(I32),
                 )
 
+        make_identity(nc, ident[:])
         idx = load_list("idx", offs)
+        nc.sync.dma_start(wgs_t[:], wgs)
         load_words(tab_w[0], tab_words[0])
         load_scale_rows(tab_s, tab_scales)
         nc.sync.dma_start(
@@ -134,34 +151,22 @@ def tile_list_welllog_marker_matcher_kernel(
         load_words(tab_w[1], tab_words[1])
         load_chunk(2)
         idx3 = load_list("idx3", offs3)
-        load_gain(0)
         load_chunk(3)
         load_page(0)
 
+        deal_gain()
         for a in range(PASSES):
             nc.vector.tensor_copy(v_w[a][:], tab_w[a][:].indirect(idx[:]))
             nc.vector.tensor_copy(v_s[a][:], tab_s[:, a, :].indirect(idx[:]))
-        nc.vector.tensor_copy(
-            w1_wd[:].rearrange("p (g t m) -> p g m t", t=PACK, m=P),
-            w1_w[:].rearrange("p (g m t) -> p g m t", t=PACK, m=P),
-        )
-        nc.vector.tensor_copy(
-            w1_sd[:].rearrange("p (g t m) -> p g m t", t=PACK, m=P),
-            w1_s[:].rearrange("p a (b m t) -> p (a b) m t", t=PACK, m=P),
-        )
-        for n in range(3):
-            quantise_chunk(n, "scalar" if n < 2 else "vector")
-        quantise_chunk(3, "vector", 0, 1)
+        for n in range(4):
+            quantise_chunk(n, rounded(n), "vector")
 
         def second_loads():
-            load_page(1)
-            load_gain(1)
             load_chunk(4)
-            load_gain(2)
-            load_page(2)
+            load_page(1)
             load_chunk(5)
             load_chunk(6)
-            load_gain(3)
+            load_page(2)
             load_chunk(7)
             load_page(3)
             load_page(4)
@@ -185,49 +190,55 @@ def tile_list_welllog_marker_matcher_kernel(
                 nc.sync.dma_start(mark_t[:], mark.rearrange("(c p) -> p c", p=P))
             return idx2, p1, p2
 
-        def product(bank, s, which):
-            b, t = s // PACK, s % PACK
+        def product(bank, b, c, which):
+            picked = slice(P * c, P * (c + 1))
             for a in range(PASSES):
                 if which == 1:
-                    cols = slice(H * a + P * s, H * a + P * (s + 1))
-                    lhs, lhs_s = w1_wd[:, cols].bitcast(FP4X4), w1_sd[:, cols]
+                    rhs = w1_w[:, H * a + PASS * b : H * a + PASS * (b + 1)].bitcast(FP4X4)
+                    rhs_s = w1_s[:, a, PASS * b : PASS * (b + 1)]
                 else:
                     n = 4 * b + 2 * (which - 2) + a
-                    cols = slice(P * t, P * (t + 1))
-                    lhs, lhs_s = w_c[n][:, cols].bitcast(FP8X4), w_s[n][:, cols]
+                    rhs, rhs_s = w_c[n][:].bitcast(FP8X4), w_s[n][:]
                 nc.tensor.matmul_mx(
-                    out=bank[:], lhsT=lhs, lhsT_scale=lhs_s, rhs=v_w[a][:].bitcast(FP8X4), rhs_scale=v_s[a][:],
-                    start=(a == 0), stop=(a == PASSES - 1),
+                    out=bank[:], lhsT=v_w[a][:, picked].bitcast(FP8X4), lhsT_scale=v_s[a][:, picked],
+                    rhs=rhs, rhs_scale=rhs_s, start=(a == 0), stop=(a == PASSES - 1),
                 )
 
-        def angle(s):
-            y2 = banks[5 if s in (1, 2, 3) else s % 2]
-            product(y2, s, 2)
-            nc.scalar.activation(feat[s], y2[:], ACT.Sin, scale=0.5)
-            nc.scalar.activation(feat[s], feat[s], ACT.Square)
+        def angles(b, sines):
+            for c in range(4):
+                y2 = banks[1 + c % 2]
+                product(y2, b, c, 2)
+                nc.scalar.activation(sines[c], y2[:], ACT.Sin, scale=0.5)
+                nc.scalar.activation(feat[c][:], sines[c], ACT.Square)
 
-        def front(s):
-            y1 = banks[2 + s % 3]
-            product(y1, s, 1)
-            nc.vector.scalar_tensor_tensor(feat[s], feat[s], 0.5, y1[:], ALU.subtract, ALU.mult)
+        def cosine_part(b, scaled):
+            for c in range(4):
+                y1 = banks[(3 + c) % 4]
+                product(y1, b, c, 1)
+                nc.vector.scalar_tensor_tensor(scaled[c], feat[c][:], 0.5, y1[:], ALU.subtract, ALU.mult)
 
-        def middle(s):
-            y3 = banks[5 + s % 3]
-            product(y3, s, 3)
-            nc.vector.scalar_tensor_tensor(feat[s], feat[s], -2.0, y3[:], ALU.mult, ALU.add)
+        def sum_part(b, scaled):
+            for c in range(4):
+                y3 = banks[4 + c]
+                product(y3, b, c, 3)
+                nc.vector.scalar_tensor_tensor(feat[c][:], scaled[c], -2.0, y3[:], ALU.mult, ALU.add)
+
+        def turn(s):
+            t = s % PACK
+            bank = banks[7 * (t % 2)]
+            for c in range(4):
+                nc.tensor.transpose(bank[:, P * c : P * (c + 1)], feat[c][:, t:PASS:PACK], ident[:])
+            nc.scalar.copy(turned[s], bank[:])
 
         def place(s):
-            nc.vector.tensor_tensor(page[s][:].indirect(idx3[:]), feat[s], gain[s % PACK][:], ALU.mult)
-
-        def reuse(name, tag, shape, dtype):
-            return keep.tile(shape, dtype, name=name, tag=tag, align_bytes=64)
+            nc.vector.tensor_tensor(page[s][:].indirect(idx3[:]), turned[s], gain[s % PACK][:], ALU.mult)
 
         def stage(t):
             for h in range(2):
                 nc.sync.dma_start(raw[h][:, t, :], page[t][:, HALF * h : HALF * (h + 1)])
 
         def quantise_page(n, src):
-            nc.vector.quantize_mx(out=page_c[n][:].bitcast(FP8X4), scales=page_s[n][:], in_=src[:])
+            nc.vector.quantize_mx(out=page_c[n][:].bitcast(FP8X4), scales=page_s[n][:], in_=src)
 
         def gather_candidates(half, tag):
             words = reuse("v2_w%d" % half, tag, [P, PASSES, S2 // 2], U32)
@@ -235,39 +246,43 @@ def tile_list_welllog_marker_matcher_kernel(
                 nc.vector.tensor_copy(words[:, a, :], tab2_w[a][:].indirect(idx2[:, 16 * half : 16 * (half + 1)]))
             v2_w.append(words)
 
-        woven = []
-        angle(0)
-        front(0)
-        middle(0)
-        quantise_chunk(3, "scalar", 1, PACK)
-        for s in range(1, PACK):
-            angle(s)
+        in_place = [tile[:] for tile in feat]
+        angles(0, in_place)
+        cosine_part(0, in_place)
+        sum_part(0, in_place)
         second_loads()
+        turn(0)
+        turn(1)
+        for n in (4, 5):
+            quantise_chunk(n, rounded(n), "scalar")
+        turned.append(reuse("turned2", "rounded_slot2", [P, S], F32)[:])
+        turned.append(sb("turned3", [P, S], F32)[:])
+        turn(2)
+        turn(3)
         for s in range(SLICES):
             if s == 3:
-                for n in range(4, 8):
-                    quantise_chunk(n, "scalar")
-                feat_late = reuse("feat_late", "raw3", [P, PACK, S], F32)
-                feat.extend([feat_late[:, t, :] for t in range(PACK)])
+                sines = reuse("sines", "late", [P, 2, PASS], F32)
+                quantise_chunk(6, rounded(6), "scalar")
+                angles(1, [sines[:, c % 2, :] for c in range(4)])
+                quantise_chunk(7, reuse("rounded7", "late", [P, PACK * HALF], BF16)[:], "scalar")
+                halves = [reuse("scaled_" + tag, tag, [P, 2, PASS], F32) for tag in ("early", "late")]
+                scaled = [halves[c // 2][:, c % 2, :] for c in range(4)]
+                cosine_part(1, scaled)
+                sum_part(1, scaled)
+                turned_late = reuse("turned_late", "raw3", [P, PACK, S], F32)
+                turned.extend([turned_late[:, t, :] for t in range(PACK)])
                 for later in range(PACK, SLICES):
-                    angle(later)
-            if s + 1 < SLICES:
-                front(s + 1)
+                    turn(later)
             place(s)
-            if s + 1 < SLICES:
-                middle(s + 1)
             if s == PACK - 1:
                 for t in range(PACK):
                     stage(t)
                 idx2, p1, p2 = third_loads()
                 for h in range(2):
-                    dst = rounded[(8 + h) % 3]
-                    nc.scalar.copy(
-                        dst[:].rearrange("p (c i t) -> p c t i", t=PACK, i=4),
-                        raw[h][:].rearrange("p t (c i) -> p c t i", i=4),
-                    )
+                    dst = reuse("rounded_page%d" % h, ("late", "early")[h], [P, PACK * HALF], BF16)[:]
+                    weave(("vector", "scalar")[h], dst, raw[h][:])
                     quantise_page(h, dst)
-                    woven.append(reuse("woven%d" % h, "raw%d" % h, [P, PACK * HALF], BF16))
+                woven = reuse("woven", "feat3", [P, 2, PACK * HALF], BF16)
             if s == SLICES - 1:
                 v2_s = reuse("v2_s", "gain3", [P, S2], U8)
                 nc.vector.tensor_copy(v2_s[:], tab2_s[:].indirect(idx2[:]))
@@ -275,20 +290,18 @@ def tile_list_welllog_marker_matcher_kernel(
             if s >= PACK:
                 for h in range(2):
                     nc.scalar.copy(
-                        woven[h][:].rearrange("p (n t) -> p n t", t=PACK)[:, :, s - PACK],
+                        woven[:, h, :].rearrange("p (n t) -> p n t", t=PACK)[:, :, s - PACK],
                         page[s][:, HALF * h : HALF * (h + 1)],
                     )
 
         for h in range(2):
-            quantise_page(2 + h, woven[h])
-        gather_candidates(1, "raw1")
+            quantise_page(2 + h, woven[:, h, :])
+        gather_candidates(1, "feat3")
 
         score_banks = ((4, 7), (0, 1), (2, 5), (3, 6))
 
         def combine(m):
-            nc.vector.scalar_tensor_tensor(
-                first[m][:], first[m][:], mark_t[:, m : m + 1], second[m % 2][:], ALU.mult, ALU.add
-            )
+            nc.vector.tensor_tensor(first[m][:], first[m][:], second[m % 2][:], ALU.add)
             nc.sync.dma_start(out[P * m : P * (m + 1), :], first[m][:])
 
         for m in range(4):
@@ -302,8 +315,9 @@ def tile_list_welllog_marker_matcher_kernel(
                         start=(a == 0), stop=(a == PASSES - 1),
                     )
                 nc.scalar.copy(score[m][:, HALF * h : HALF * (h + 1)], bank[:])
-            nc.vector.tensor_tensor(second[m % 2][:], score[m][:].indirect(p2[:]), tie_t[:, m, :], ALU.mult)
+            nc.vector.tensor_copy(first[m][:], score[m][:].indirect(p1[:]))
+            nc.scalar.activation(first[m][:], first[m][:], ACT.Copy, scale=mark_t[:, m : m + 1])
             if m > 0:
                 combine(m - 1)
-            nc.vector.tensor_copy(first[m][:], score[m][:].indirect(p1[:]))
+            nc.vector.tensor_tensor(second[m % 2][:], score[m][:].indirect(p2[:]), tie_t[:, m, :], ALU.mult)
         combine(3)

@@ -14,13 +14,17 @@ FP4X4 = mybir.dt.float4_e2m1fn_x4
 ALU = mybir.AluOpType
 ACT = mybir.ActivationFunctionType
 
+K, T, S, H, S2, T3, T2, PAIRS = 1024, 2048, 512, 1024, 512, 2048, 1024, 512
 P = 128
+QUAD = 32
 PACK = 4
 PASS = P * PACK
-K, T, S, H, S2, T3, T2, PAIRS = 1024, 2048, 512, 1024, 512, 2048, 1024, 512
 PASSES = 2
 SLICES = H // P
-HALF = 512
+BANK = 512
+TILES = 4
+LIST_COLS = S // 16
+SUMMED_ON_TENSOR = 2
 FLOPS = 2 * (3 * K * H * S + H * S2 * T2)
 
 
@@ -34,57 +38,71 @@ def tile_list_welllog_marker_matcher_kernel(
         keep = ctx.enter_context(tc.tile_pool(name="keep", bufs=1))
         psum = ctx.enter_context(tc.psum_pool(name="psum", bufs=1))
 
-        def sb(name, shape, dtype):
-            return keep.tile(shape, dtype, name=name, tag=name, align_bytes=64)
-
-        def reuse(name, tag, shape, dtype):
+        def tile_on(name, tag, shape, dtype):
             return keep.tile(shape, dtype, name=name, tag=tag, align_bytes=64)
 
-        def many(name, count, shape, dtype):
-            return [sb("%s%d" % (name, i), shape, dtype) for i in range(count)]
+        def own_tile(name, shape, dtype):
+            return tile_on(name, name, shape, dtype)
+
+        def own_tiles(name, count, shape, dtype):
+            return [own_tile("%s%d" % (name, i), shape, dtype) for i in range(count)]
+
+        def block(i):
+            return slice(P * i, P * (i + 1))
+
+        banks = [psum.tile([P, BANK], F32, name="bank%d" % i) for i in range(8)]
+
+        tab_w = own_tiles("tab_w", PASSES, [P, T], U32)
+        tab_s = own_tile("tab_s", [P, PASSES, T], U8)
+        tab2_w = own_tiles("tab2_w", PASSES, [P, T3], U32)
+        tab2_s = own_tile("tab2_s", [P, T3], U8)
+        v_w = own_tiles("v_w", PASSES, [P, S], U32)
+        v_s = own_tiles("v_s", PASSES, [P, S], U8)
+        w1_w = own_tile("w1_w", [P, PASSES * H], U16)
+        w1_s = own_tile("w1_s", [P, PASSES, H], U8)
+        raw = own_tiles("raw", 4, [P, PACK, BANK], F32)
+        chunk_w = own_tiles("chunk_w", 8, [P, BANK], U32)
+        chunk_s = own_tiles("chunk_s", 8, [P, BANK], U8)
+        page = own_tiles("page", SLICES, [P, T2], F32)
+        page_w = own_tiles("page_w", 2 * PASSES, [P, BANK], U32)
+        page_s = own_tiles("page_s", 2 * PASSES, [P, BANK], U8)
+        feat = own_tiles("feat", TILES, [P, PASS], F32)
+        turned = [tile[:] for tile in own_tiles("turned", 2, [P, S], F32)]
+        gain = own_tiles("gain", PACK, [P, S], F32)
+        ident = own_tile("ident", [P, P], F32)
+        wgs_rows = tile_on("wgs_rows", "early", [P, S], F32)
+        wgs_turned = tile_on("wgs_turned", "late", [P, PACK, TILES * P], F32)
+        score = own_tiles("score", TILES, [P, T2], F32)
+        tie_rows = own_tile("tie_rows", [P, TILES, PAIRS], F32)
+        mark_rows = own_tile("mark_rows", [P, TILES], F32)
+        first = own_tiles("first", TILES, [P, PAIRS], F32)
+        second = own_tiles("second", TILES, [P, PAIRS], F32)
 
         def load_list(name, src):
-            tile = lists.tile([P, 32], U16, name=name)
+            tile = lists.tile([P, LIST_COLS], U16, name=name)
             nc.sync.dma_start(tile[:], src)
             return tile
 
-        banks = [psum.tile([P, HALF], F32, name="bank%d" % i) for i in range(8)]
-
-        tab_w = many("tab_w", PASSES, [P, T], U32)
-        tab_s = sb("tab_s", [P, PASSES, T], U8)
-        tab2_w = many("tab2_w", PASSES, [P, T3], U32)
-        tab2_s = sb("tab2_s", [P, T3], U8)
-        v_w = many("v_w", PASSES, [P, S], U32)
-        v_s = many("v_s", PASSES, [P, S], U8)
-        v2_w = []
-        w1_w = sb("w1_w", [P, PASSES * H], U16)
-        w1_s = sb("w1_s", [P, PASSES, H], U8)
-        raw = many("raw", 4, [P, PACK, HALF], F32)
-        w_c = many("w_c", 8, [P, HALF], U32)
-        w_s = many("w_s", 8, [P, HALF], U8)
-        page = many("page", SLICES, [P, T2], F32)
-        page_c = many("page_c", 4, [P, HALF], U32)
-        page_s = many("page_s", 4, [P, HALF], U8)
-        feat = many("feat", 4, [P, PASS], F32)
-        turned = [tile[:] for tile in many("turned", 2, [P, S], F32)]
-        gain = many("gain", PACK, [P, S], F32)
-        ident = sb("ident", [P, P], F32)
-        wgs_t = reuse("wgs_t", "early", [P, S], F32)
-        wgs_turned = reuse("wgs_turned", "late", [P, 4, PACK * P], F32)
-        score = many("score", 4, [P, T2], F32)
-        tie_t = sb("tie_t", [P, 4, PAIRS], F32)
-        mark_t = sb("mark_t", [P, 4], F32)
-        first = many("first", 4, [P, PAIRS], F32)
-        second = many("second", 2, [P, PAIRS], F32)
-
         def load_words(tile, words):
             nc.sync.dma_start(tile[:].bitcast(I32), words.rearrange("p t i -> p (t i)").bitcast(I32))
+
+        def load_scale_rows(dst, src):
+            for r in range(4):
+                nc.sync.dma_start(
+                    dst[r:P:QUAD].bitcast(I32),
+                    src[:, r:16:4, :].rearrange("a q t -> q a t").bitcast(I32),
+                )
 
         def load_chunk(n):
             b, a = n // 4, n % 2
             w = w2 if n % 4 < 2 else w3
             src = w[PASS * a : PASS * (a + 1), PASS * b : PASS * (b + 1)]
             nc.sync.dma_start(raw[n % 4][:], src.rearrange("(p j) c -> p j c", j=PACK))
+
+        page_rows = page0.rearrange("(b p t) n -> b t p n", p=P, t=PACK)
+
+        def load_page(s):
+            nc.sync.dma_start(page[s][:], page_rows[s // PACK, s % PACK])
 
         def copy_on(engine, dst, src):
             if engine == "scalar":
@@ -99,56 +117,100 @@ def tile_list_welllog_marker_matcher_kernel(
                 src.rearrange("p t (c i) -> p c t i", i=2),
             )
 
+        def rounded_on(name, tag):
+            return tile_on(name, tag, [P, PACK * BANK], BF16)[:]
+
         def rounded(n):
-            return reuse("rounded%d" % n, "rounded_slot%d" % (n % 3), [P, PACK * HALF], BF16)[:]
+            return rounded_on("rounded%d" % n, "rounded_slot%d" % (n % 3))
 
         def quantise_chunk(n, dst, engine):
             weave(engine, dst, raw[n % 4][:])
-            nc.vector.quantize_mx(out=w_c[n][:].bitcast(FP8X4), scales=w_s[n][:], in_=dst)
-
-        page_rows = page0.rearrange("(b p t) n -> b t p n", p=P, t=PACK)
-
-        def load_page(s):
-            nc.sync.dma_start(page[s][:], page_rows[s // PACK, s % PACK])
+            nc.vector.quantize_mx(out=chunk_w[n][:].bitcast(FP8X4), scales=chunk_s[n][:], in_=dst)
 
         def deal_gain():
-            for c in range(4):
-                nc.tensor.transpose(banks[7][:, P * c : P * (c + 1)], wgs_t[:, P * c : P * (c + 1)], ident[:])
-            rows = banks[7][:].rearrange("p (c q t) -> p t c q", c=4, t=PACK)
+            for c in range(TILES):
+                nc.tensor.transpose(banks[7][:, block(c)], wgs_rows[:, block(c)], ident[:])
+            rows = banks[7][:].rearrange("p (c q t) -> p t c q", c=TILES, t=PACK)
             for t in range(PACK):
                 nc.scalar.copy(
-                    wgs_turned[:, t, :].rearrange("p (c g q) -> p c g q", c=4, g=4),
-                    rows[:, t].unsqueeze(2).to_broadcast([P, 4, 4, 32]),
+                    wgs_turned[:, t, :].rearrange("p (c g q) -> p c g q", c=TILES, q=QUAD),
+                    rows[:, t].unsqueeze(2).to_broadcast([P, TILES, P // QUAD, QUAD]),
                 )
             for t in range(PACK):
                 bank = banks[(6, 4, 1, 7)[t]]
-                for c in range(4):
-                    nc.tensor.transpose(bank[:, P * c : P * (c + 1)], wgs_turned[:, t, P * c : P * (c + 1)], ident[:])
+                for c in range(TILES):
+                    nc.tensor.transpose(bank[:, block(c)], wgs_turned[:, t, block(c)], ident[:])
                 nc.scalar.copy(gain[t][:], bank[:])
+
+        def product(bank, b, c, weight):
+            for a in range(PASSES):
+                if weight == "w1":
+                    rhs = w1_w[:, H * a + PASS * b : H * a + PASS * (b + 1)].bitcast(FP4X4)
+                    rhs_s = w1_s[:, a, PASS * b : PASS * (b + 1)]
+                else:
+                    n = 4 * b + (0 if weight == "w2" else 2) + a
+                    rhs, rhs_s = chunk_w[n][:].bitcast(FP8X4), chunk_s[n][:]
+                nc.tensor.matmul_mx(
+                    out=bank[:], lhsT=v_w[a][:, block(c)].bitcast(FP8X4), lhsT_scale=v_s[a][:, block(c)],
+                    rhs=rhs, rhs_scale=rhs_s, start=(a == 0), stop=(a == PASSES - 1),
+                )
+
+        def angles(b, sines):
+            for c in range(TILES):
+                y2 = banks[(4, 5, 6, 1)[c]]
+                product(y2, b, c, "w2")
+                nc.scalar.activation(sines[c], y2[:], ACT.Sin, scale=0.5)
+                nc.scalar.activation(feat[c][:], sines[c], ACT.Square)
+
+        def cosine_part(b, scaled):
+            for c in range(TILES):
+                y1 = banks[(2, 3, 0, 1)[c]]
+                product(y1, b, c, "w1")
+                nc.vector.scalar_tensor_tensor(scaled[c], feat[c][:], 0.5, y1[:], ALU.subtract, ALU.mult)
+
+        def sum_part(b, scaled):
+            for c in range(TILES):
+                y3 = banks[4 + c]
+                product(y3, b, c, "w3")
+                nc.vector.scalar_tensor_tensor(feat[c][:], scaled[c], -2.0, y3[:], ALU.mult, ALU.add)
+
+        def turn(s):
+            t = s % PACK
+            bank = banks[7 * (t % 2)]
+            for c in range(TILES):
+                nc.tensor.transpose(bank[:, block(c)], feat[c][:, t:PASS:PACK], ident[:])
+            copy_on("vector" if s == 0 else "scalar", turned[s], bank[:])
+
+        def place(s):
+            nc.vector.tensor_tensor(page[s][:].indirect(idx3[:]), turned[s], gain[s % PACK][:], ALU.mult)
+
+        def quantise_page(n, src):
+            nc.vector.quantize_mx(out=page_w[n][:].bitcast(FP8X4), scales=page_s[n][:], in_=src)
+
+        def gather_candidates(half, tag):
+            words = tile_on("v2_w%d" % half, tag, [P, PASSES, S2 // 2], U32)
+            entries = idx2[:, LIST_COLS // 2 * half : LIST_COLS // 2 * (half + 1)]
+            for a in range(PASSES):
+                nc.vector.tensor_copy(words[:, a, :], tab2_w[a][:].indirect(entries))
+            return words
 
         nc.vector.memset(tab_s[:].rearrange("p a t -> p (a t)").bitcast(I32), 0)
         nc.vector.memset(w1_s[:].rearrange("p a t -> p (a t)").bitcast(I32), 0)
         nc.vector.memset(tab2_s[:].bitcast(I32), 0)
-        def load_scale_rows(dst, src):
-            for r in range(4):
-                nc.sync.dma_start(
-                    dst[r:P:32].bitcast(I32),
-                    src[:, r:16:4, :].rearrange("a q t -> q a t").bitcast(I32),
-                )
-
         make_identity(nc, ident[:])
+
         idx = load_list("idx", offs)
-        nc.sync.dma_start(wgs_t[:], wgs)
+        nc.sync.dma_start(wgs_rows[:], wgs)
         load_words(tab_w[0], tab_words[0])
         load_scale_rows(tab_s, tab_scales)
+        load_chunk(0)
+        load_words(tab_w[1], tab_words[1])
+        load_scale_rows(w1_s, w1_scales)
+        load_chunk(1)
         nc.sync.dma_start(
             w1_w[:].bitcast(I32).rearrange("p (a c) -> p a c", a=PASSES),
             w1_words.rearrange("a p c -> p a c").bitcast(I32),
         )
-        load_chunk(0)
-        load_scale_rows(w1_s, w1_scales)
-        load_chunk(1)
-        load_words(tab_w[1], tab_words[1])
         load_chunk(2)
         idx3 = load_list("idx3", offs3)
         load_chunk(3)
@@ -158,166 +220,130 @@ def tile_list_welllog_marker_matcher_kernel(
         for a in range(PASSES):
             nc.vector.tensor_copy(v_w[a][:], tab_w[a][:].indirect(idx[:]))
             nc.vector.tensor_copy(v_s[a][:], tab_s[:, a, :].indirect(idx[:]))
-        for n in range(4):
+
+        for n in range(3):
             quantise_chunk(n, rounded(n), "vector")
+        quantise_chunk(3, rounded_on("rounded3", "tab_w0"), "vector")
+        angles(0, [tile[:] for tile in feat])
+        scaled_tile = tile_on("scaled_pass0", "tab_w0", [P, TILES, PASS], F32)
+        scaled = [scaled_tile[:, c, :] for c in range(TILES)]
+        cosine_part(0, scaled)
+        sum_part(0, scaled)
 
-        def second_loads():
-            load_chunk(4)
-            load_page(1)
-            load_chunk(5)
-            load_chunk(6)
-            load_page(2)
-            load_chunk(7)
-            load_page(3)
-            load_page(4)
+        for n in (4, 5, 6):
+            load_chunk(n)
+        for s in (1, 2):
+            load_page(s)
+        load_chunk(7)
+        for s in (3, 4):
+            load_page(s)
 
-        def third_loads():
-            load_page(5)
-            load_page(6)
-            idx2 = load_list("idx2", offs2)
-            for a in range(PASSES):
-                load_words(tab2_w[a], tab2_words[a])
-            for quad in range(4):
-                nc.sync.dma_start(
-                    tab2_s[32 * quad : 32 * quad + 8, :].bitcast(I32),
-                    tab2_scales[:, 4 * quad : 4 * quad + 4, :].bitcast(I32),
-                )
-            load_page(7)
-            nc.sync.dma_start(tie_t[:], tie.rearrange("(c p) j -> p c j", p=P))
-            p1 = load_list("p1", pos1)
-            p2 = load_list("p2", pos2)
-            with nc.allow_non_contiguous_dma("one value of mark for each partition and row tile"):
-                nc.sync.dma_start(mark_t[:], mark.rearrange("(c p) -> p c", p=P))
-            return idx2, p1, p2
-
-        def product(bank, b, c, which):
-            picked = slice(P * c, P * (c + 1))
-            for a in range(PASSES):
-                if which == 1:
-                    rhs = w1_w[:, H * a + PASS * b : H * a + PASS * (b + 1)].bitcast(FP4X4)
-                    rhs_s = w1_s[:, a, PASS * b : PASS * (b + 1)]
-                else:
-                    n = 4 * b + 2 * (which - 2) + a
-                    rhs, rhs_s = w_c[n][:].bitcast(FP8X4), w_s[n][:]
-                nc.tensor.matmul_mx(
-                    out=bank[:], lhsT=v_w[a][:, picked].bitcast(FP8X4), lhsT_scale=v_s[a][:, picked],
-                    rhs=rhs, rhs_scale=rhs_s, start=(a == 0), stop=(a == PASSES - 1),
-                )
-
-        def angles(b, sines):
-            for c in range(4):
-                y2 = banks[1 + c % 2]
-                product(y2, b, c, 2)
-                nc.scalar.activation(sines[c], y2[:], ACT.Sin, scale=0.5)
-                nc.scalar.activation(feat[c][:], sines[c], ACT.Square)
-
-        def cosine_part(b, scaled):
-            for c in range(4):
-                y1 = banks[(3 + c) % 4]
-                product(y1, b, c, 1)
-                nc.vector.scalar_tensor_tensor(scaled[c], feat[c][:], 0.5, y1[:], ALU.subtract, ALU.mult)
-
-        def sum_part(b, scaled):
-            for c in range(4):
-                y3 = banks[4 + c]
-                product(y3, b, c, 3)
-                nc.vector.scalar_tensor_tensor(feat[c][:], scaled[c], -2.0, y3[:], ALU.mult, ALU.add)
-
-        def turn(s):
-            t = s % PACK
-            bank = banks[7 * (t % 2)]
-            for c in range(4):
-                nc.tensor.transpose(bank[:, P * c : P * (c + 1)], feat[c][:, t:PASS:PACK], ident[:])
-            nc.scalar.copy(turned[s], bank[:])
-
-        def place(s):
-            nc.vector.tensor_tensor(page[s][:].indirect(idx3[:]), turned[s], gain[s % PACK][:], ALU.mult)
-
-        def stage(t):
-            for h in range(2):
-                nc.sync.dma_start(raw[h][:, t, :], page[t][:, HALF * h : HALF * (h + 1)])
-
-        def quantise_page(n, src):
-            nc.vector.quantize_mx(out=page_c[n][:].bitcast(FP8X4), scales=page_s[n][:], in_=src)
-
-        def gather_candidates(half, tag):
-            words = reuse("v2_w%d" % half, tag, [P, PASSES, S2 // 2], U32)
-            for a in range(PASSES):
-                nc.vector.tensor_copy(words[:, a, :], tab2_w[a][:].indirect(idx2[:, 16 * half : 16 * (half + 1)]))
-            v2_w.append(words)
-
-        in_place = [tile[:] for tile in feat]
-        angles(0, in_place)
-        cosine_part(0, in_place)
-        sum_part(0, in_place)
-        second_loads()
         turn(0)
         turn(1)
         for n in (4, 5):
             quantise_chunk(n, rounded(n), "scalar")
-        turned.append(reuse("turned2", "rounded_slot2", [P, S], F32)[:])
-        turned.append(sb("turned3", [P, S], F32)[:])
+        turned.append(tile_on("turned2", "rounded_slot2", [P, S], F32)[:])
+        turned.append(own_tile("turned3", [P, S], F32)[:])
         turn(2)
         turn(3)
-        for s in range(SLICES):
-            if s == 3:
-                sines = reuse("sines", "late", [P, 2, PASS], F32)
-                quantise_chunk(6, rounded(6), "scalar")
-                angles(1, [sines[:, c % 2, :] for c in range(4)])
-                quantise_chunk(7, reuse("rounded7", "late", [P, PACK * HALF], BF16)[:], "scalar")
-                halves = [reuse("scaled_" + tag, tag, [P, 2, PASS], F32) for tag in ("early", "late")]
-                scaled = [halves[c // 2][:, c % 2, :] for c in range(4)]
-                cosine_part(1, scaled)
-                sum_part(1, scaled)
-                turned_late = reuse("turned_late", "raw3", [P, PACK, S], F32)
-                turned.extend([turned_late[:, t, :] for t in range(PACK)])
-                for later in range(PACK, SLICES):
-                    turn(later)
+        for s in range(PACK - 1):
             place(s)
-            if s == PACK - 1:
-                for t in range(PACK):
-                    stage(t)
-                idx2, p1, p2 = third_loads()
-                for h in range(2):
-                    dst = reuse("rounded_page%d" % h, ("late", "early")[h], [P, PACK * HALF], BF16)[:]
-                    weave(("vector", "scalar")[h], dst, raw[h][:])
-                    quantise_page(h, dst)
-                woven = reuse("woven", "feat3", [P, 2, PACK * HALF], BF16)
-            if s == SLICES - 1:
-                v2_s = reuse("v2_s", "gain3", [P, S2], U8)
-                nc.vector.tensor_copy(v2_s[:], tab2_s[:].indirect(idx2[:]))
-                gather_candidates(0, "raw3")
-            if s >= PACK:
-                for h in range(2):
-                    nc.scalar.copy(
-                        woven[:, h, :].rearrange("p (n t) -> p n t", t=PACK)[:, :, s - PACK],
-                        page[s][:, HALF * h : HALF * (h + 1)],
-                    )
 
-        for h in range(2):
-            quantise_page(2 + h, woven[:, h, :])
-        gather_candidates(1, "feat3")
+        sines = tile_on("sines", "late", [P, 2, PASS], F32)
+        quantise_chunk(6, rounded(6), "scalar")
+        angles(1, [sines[:, c % 2, :] for c in range(TILES)])
+        quantise_chunk(7, rounded_on("rounded7", "late"), "scalar")
+        halves = [tile_on("scaled_" + tag, tag, [P, 2, PASS], F32) for tag in ("early", "late")]
+        scaled = [halves[c // 2][:, c % 2, :] for c in range(TILES)]
+        cosine_part(1, scaled)
+        sum_part(1, scaled)
+        turned_late = tile_on("turned_late", "raw3", [P, PACK, S], F32)
+        turned.extend([turned_late[:, t, :] for t in range(PACK)])
+        for s in range(PACK, SLICES):
+            turn(s)
+        place(PACK - 1)
+
+        for t in range(PACK):
+            for u in range(2):
+                nc.sync.dma_start(raw[u][:, t, :], page[t][:, BANK * u : BANK * (u + 1)])
+
+        for s in (5, 6):
+            load_page(s)
+        idx2 = load_list("idx2", offs2)
+        for a in range(PASSES):
+            load_words(tab2_w[a], tab2_words[a])
+        for quad in range(P // QUAD):
+            nc.sync.dma_start(
+                tab2_s[QUAD * quad : QUAD * quad + 4 * PASSES, :].bitcast(I32),
+                tab2_scales[:, 4 * quad : 4 * quad + 4, :].bitcast(I32),
+            )
+        load_page(7)
+        nc.sync.dma_start(tie_rows[:], tie.rearrange("(c p) j -> p c j", p=P))
+        p1 = load_list("p1", pos1)
+        p2 = load_list("p2", pos2)
+        with nc.allow_non_contiguous_dma("one value of mark for each partition and row tile"):
+            nc.sync.dma_start(mark_rows[:], mark.rearrange("(c p) -> p c", p=P))
+
+        for u, (tag, engine) in enumerate((("late", "vector"), ("early", "scalar"))):
+            dst = rounded_on("rounded_page%d" % u, tag)
+            weave(engine, dst, raw[u][:])
+            quantise_page(u, dst)
+
+        woven = tile_on("woven", "feat3", [P, 2, PACK * BANK], BF16)
+        for s in range(PACK, SLICES):
+            place(s)
+            if s == SLICES - 1:
+                v2_s = tile_on("v2_s", "gain3", [P, S2], U8)
+                nc.vector.tensor_copy(v2_s[:], tab2_s[:].indirect(idx2[:]))
+                v2_w = [gather_candidates(0, "raw3")]
+            for u in range(2):
+                nc.scalar.copy(
+                    woven[:, u, :].rearrange("p (n t) -> p n t", t=PACK)[:, :, s - PACK],
+                    page[s][:, BANK * u : BANK * (u + 1)],
+                )
+        for u in range(2):
+            quantise_page(2 + u, woven[:, u, :])
+        v2_w.append(gather_candidates(1, "feat3"))
 
         score_banks = ((4, 7), (0, 1), (2, 5), (3, 6))
-
-        def combine(m):
-            nc.vector.tensor_tensor(first[m][:], first[m][:], second[m % 2][:], ALU.add)
-            nc.sync.dma_start(out[P * m : P * (m + 1), :], first[m][:])
-
-        for m in range(4):
-            cols = slice(P * (m % 2), P * (m % 2 + 1))
-            for h in range(2):
-                bank = banks[score_banks[m][h]]
+        for m in range(TILES):
+            for u in range(2):
+                bank = banks[score_banks[m][u]]
                 for a in range(PASSES):
                     nc.tensor.matmul_mx(
-                        out=bank[:], lhsT=v2_w[m // 2][:, a, cols].bitcast(FP8X4), lhsT_scale=v2_s[4 * a : P, P * m : P * (m + 1)],
-                        rhs=page_c[2 * a + h][:].bitcast(FP8X4), rhs_scale=page_s[2 * a + h][:],
+                        out=bank[:],
+                        lhsT=v2_w[m // 2][:, a, block(m % 2)].bitcast(FP8X4), lhsT_scale=v2_s[4 * a : P, block(m)],
+                        rhs=page_w[2 * a + u][:].bitcast(FP8X4), rhs_scale=page_s[2 * a + u][:],
                         start=(a == 0), stop=(a == PASSES - 1),
                     )
-                nc.scalar.copy(score[m][:, HALF * h : HALF * (h + 1)], bank[:])
+                nc.scalar.copy(score[m][:, BANK * u : BANK * (u + 1)], bank[:])
+
+        def combine(m):
+            if m < SUMMED_ON_TENSOR:
+                sum_bank, back_bank = banks[score_banks[m][0]], banks[score_banks[m][1]]
+                for c in range(TILES):
+                    for term, opens in ((first[m], True), (second[m], False)):
+                        nc.tensor.matmul(
+                            sum_bank[:, block(c)], term[:, block(c)], ident[:],
+                            start=opens, stop=not opens, is_transpose=True,
+                        )
+                sum_turned = tile_on("sum_turned%d" % m, "feat%d" % m, [P, PAIRS], F32)
+                nc.scalar.copy(sum_turned[:], sum_bank[:])
+                for c in range(TILES):
+                    nc.tensor.transpose(back_bank[:, block(c)], sum_turned[:, block(c)], ident[:])
+                nc.scalar.copy(first[m][:], back_bank[:])
+                nc.scalar.dma_start(out[block(m), :], first[m][:])
+            else:
+                nc.vector.scalar_tensor_tensor(
+                    first[m][:], first[m][:], mark_rows[:, m : m + 1], second[m][:], ALU.mult, ALU.add
+                )
+                nc.sync.dma_start(out[block(m), :], first[m][:])
+
+        for m in range(TILES):
             nc.vector.tensor_copy(first[m][:], score[m][:].indirect(p1[:]))
-            nc.scalar.activation(first[m][:], first[m][:], ACT.Copy, scale=mark_t[:, m : m + 1])
+            if m < SUMMED_ON_TENSOR:
+                nc.scalar.activation(first[m][:], first[m][:], ACT.Copy, scale=mark_rows[:, m : m + 1])
             if m > 0:
                 combine(m - 1)
-            nc.vector.tensor_tensor(second[m % 2][:], score[m][:].indirect(p2[:]), tie_t[:, m, :], ALU.mult)
-        combine(3)
+            nc.vector.tensor_tensor(second[m][:], score[m][:].indirect(p2[:]), tie_rows[:, m, :], ALU.mult)
+        combine(TILES - 1)

from contextlib import ExitStack

import concourse.mybir as mybir
from concourse.masks import make_identity

F32 = mybir.dt.float32
BF16 = mybir.dt.bfloat16
I32 = mybir.dt.int32
U32 = mybir.dt.uint32
U16 = mybir.dt.uint16
U8 = mybir.dt.uint8
FP8X4 = mybir.dt.float8_e4m3fn_x4
FP4X4 = mybir.dt.float4_e2m1fn_x4
ALU = mybir.AluOpType
ACT = mybir.ActivationFunctionType

K, T, S, H, S2, T3, T2, PAIRS = 1024, 2048, 512, 1024, 512, 2048, 1024, 512
P = 128
QUAD = 32
PACK = 4
PASS = P * PACK
PASSES = 2
SLICES = H // P
BANK = 512
TILES = 4
LIST_COLS = S // 16
SUMMED_ON_TENSOR = 2
FLOPS = 2 * (3 * K * H * S + H * S2 * T2)


def tile_list_welllog_marker_matcher_kernel(
    tc, tab_words, tab_scales, tab2_words, tab2_scales, offs, offs2, offs3, pos1, pos2,
    w1_words, w1_scales, w2, w3, page0, wgs, mark, tie, out,
):
    nc = tc.nc
    with ExitStack() as ctx:
        lists = ctx.enter_context(tc.tile_pool(name="lists", bufs=1))
        keep = ctx.enter_context(tc.tile_pool(name="keep", bufs=1))
        psum = ctx.enter_context(tc.psum_pool(name="psum", bufs=1))

        def tile_on(name, tag, shape, dtype):
            return keep.tile(shape, dtype, name=name, tag=tag, align_bytes=64)

        def own_tile(name, shape, dtype):
            return tile_on(name, name, shape, dtype)

        def own_tiles(name, count, shape, dtype):
            return [own_tile("%s%d" % (name, i), shape, dtype) for i in range(count)]

        def block(i):
            return slice(P * i, P * (i + 1))

        banks = [psum.tile([P, BANK], F32, name="bank%d" % i) for i in range(8)]

        tab_w = own_tiles("tab_w", PASSES, [P, T], U32)
        tab_s = own_tile("tab_s", [P, PASSES, T], U8)
        tab2_w = own_tiles("tab2_w", PASSES, [P, T3], U32)
        tab2_s = own_tile("tab2_s", [P, T3], U8)
        v_w = own_tiles("v_w", PASSES, [P, S], U32)
        v_s = own_tiles("v_s", PASSES, [P, S], U8)
        w1_w = own_tile("w1_w", [P, PASSES * H], U16)
        w1_s = own_tile("w1_s", [P, PASSES, H], U8)
        raw = own_tiles("raw", 4, [P, PACK, BANK], F32)
        chunk_w = own_tiles("chunk_w", 8, [P, BANK], U32)
        chunk_s = own_tiles("chunk_s", 8, [P, BANK], U8)
        page = own_tiles("page", SLICES, [P, T2], F32)
        page_w = own_tiles("page_w", 2 * PASSES, [P, BANK], U32)
        page_s = own_tiles("page_s", 2 * PASSES, [P, BANK], U8)
        feat = own_tiles("feat", TILES, [P, PASS], F32)
        turned = [tile[:] for tile in own_tiles("turned", 2, [P, S], F32)]
        gain = own_tiles("gain", PACK, [P, S], F32)
        ident = own_tile("ident", [P, P], F32)
        wgs_rows = tile_on("wgs_rows", "early", [P, S], F32)
        wgs_turned = tile_on("wgs_turned", "late", [P, PACK, TILES * P], F32)
        score = own_tiles("score", TILES, [P, T2], F32)
        tie_rows = own_tile("tie_rows", [P, TILES, PAIRS], F32)
        mark_rows = own_tile("mark_rows", [P, TILES], F32)
        first = own_tiles("first", TILES, [P, PAIRS], F32)
        second = own_tiles("second", TILES, [P, PAIRS], F32)

        def load_list(name, src):
            tile = lists.tile([P, LIST_COLS], U16, name=name)
            nc.sync.dma_start(tile[:], src)
            return tile

        def load_words(tile, words):
            nc.sync.dma_start(tile[:].bitcast(I32), words.rearrange("p t i -> p (t i)").bitcast(I32))

        def load_scale_rows(dst, src):
            for r in range(4):
                nc.sync.dma_start(
                    dst[r:P:QUAD].bitcast(I32),
                    src[:, r:16:4, :].rearrange("a q t -> q a t").bitcast(I32),
                )

        def load_chunk(n):
            b, a = n // 4, n % 2
            w = w2 if n % 4 < 2 else w3
            src = w[PASS * a : PASS * (a + 1), PASS * b : PASS * (b + 1)]
            nc.sync.dma_start(raw[n % 4][:], src.rearrange("(p j) c -> p j c", j=PACK))

        page_rows = page0.rearrange("(b p t) n -> b t p n", p=P, t=PACK)

        def load_page(s):
            nc.sync.dma_start(page[s][:], page_rows[s // PACK, s % PACK])

        def copy_on(engine, dst, src):
            if engine == "scalar":
                nc.scalar.copy(dst, src)
            else:
                nc.vector.tensor_copy(dst, src)

        def weave(engine, dst, src):
            copy_on(
                engine,
                dst.rearrange("p (c i t) -> p c t i", t=PACK, i=2),
                src.rearrange("p t (c i) -> p c t i", i=2),
            )

        def rounded_on(name, tag):
            return tile_on(name, tag, [P, PACK * BANK], BF16)[:]

        def rounded(n):
            return rounded_on("rounded%d" % n, "rounded_slot%d" % (n % 3))

        def quantise_chunk(n, dst, engine):
            weave(engine, dst, raw[n % 4][:])
            nc.vector.quantize_mx(out=chunk_w[n][:].bitcast(FP8X4), scales=chunk_s[n][:], in_=dst)

        def deal_gain():
            for c in range(TILES):
                nc.tensor.transpose(banks[7][:, block(c)], wgs_rows[:, block(c)], ident[:])
            rows = banks[7][:].rearrange("p (c q t) -> p t c q", c=TILES, t=PACK)
            for t in range(PACK):
                nc.scalar.copy(
                    wgs_turned[:, t, :].rearrange("p (c g q) -> p c g q", c=TILES, q=QUAD),
                    rows[:, t].unsqueeze(2).to_broadcast([P, TILES, P // QUAD, QUAD]),
                )
            for t in range(PACK):
                bank = banks[(6, 4, 1, 7)[t]]
                for c in range(TILES):
                    nc.tensor.transpose(bank[:, block(c)], wgs_turned[:, t, block(c)], ident[:])
                nc.scalar.copy(gain[t][:], bank[:])

        def product(bank, b, c, weight):
            for a in range(PASSES):
                if weight == "w1":
                    rhs = w1_w[:, H * a + PASS * b : H * a + PASS * (b + 1)].bitcast(FP4X4)
                    rhs_s = w1_s[:, a, PASS * b : PASS * (b + 1)]
                else:
                    n = 4 * b + (0 if weight == "w2" else 2) + a
                    rhs, rhs_s = chunk_w[n][:].bitcast(FP8X4), chunk_s[n][:]
                nc.tensor.matmul_mx(
                    out=bank[:], lhsT=v_w[a][:, block(c)].bitcast(FP8X4), lhsT_scale=v_s[a][:, block(c)],
                    rhs=rhs, rhs_scale=rhs_s, start=(a == 0), stop=(a == PASSES - 1),
                )

        def angles(b, sines):
            for c in range(TILES):
                y2 = banks[(4, 5, 6, 1)[c]]
                product(y2, b, c, "w2")
                nc.scalar.activation(sines[c], y2[:], ACT.Sin, scale=0.5)
                nc.scalar.activation(feat[c][:], sines[c], ACT.Square)

        def cosine_part(b, scaled):
            for c in range(TILES):
                y1 = banks[(2, 3, 0, 1)[c]]
                product(y1, b, c, "w1")
                nc.vector.scalar_tensor_tensor(scaled[c], feat[c][:], 0.5, y1[:], ALU.subtract, ALU.mult)

        def sum_part(b, scaled):
            for c in range(TILES):
                y3 = banks[4 + c]
                product(y3, b, c, "w3")
                nc.vector.scalar_tensor_tensor(feat[c][:], scaled[c], -2.0, y3[:], ALU.mult, ALU.add)

        def turn(s):
            t = s % PACK
            bank = banks[7 * (t % 2)]
            for c in range(TILES):
                nc.tensor.transpose(bank[:, block(c)], feat[c][:, t:PASS:PACK], ident[:])
            copy_on("vector" if s == 0 else "scalar", turned[s], bank[:])

        def place(s):
            nc.vector.tensor_tensor(page[s][:].indirect(idx3[:]), turned[s], gain[s % PACK][:], ALU.mult)

        def quantise_page(n, src):
            nc.vector.quantize_mx(out=page_w[n][:].bitcast(FP8X4), scales=page_s[n][:], in_=src)

        def gather_candidates(half, tag):
            words = tile_on("v2_w%d" % half, tag, [P, PASSES, S2 // 2], U32)
            entries = idx2[:, LIST_COLS // 2 * half : LIST_COLS // 2 * (half + 1)]
            for a in range(PASSES):
                nc.vector.tensor_copy(words[:, a, :], tab2_w[a][:].indirect(entries))
            return words

        nc.vector.memset(tab_s[:].rearrange("p a t -> p (a t)").bitcast(I32), 0)
        nc.vector.memset(w1_s[:].rearrange("p a t -> p (a t)").bitcast(I32), 0)
        nc.vector.memset(tab2_s[:].bitcast(I32), 0)
        make_identity(nc, ident[:])

        idx = load_list("idx", offs)
        nc.sync.dma_start(wgs_rows[:], wgs)
        load_words(tab_w[0], tab_words[0])
        load_scale_rows(tab_s, tab_scales)
        load_chunk(0)
        load_words(tab_w[1], tab_words[1])
        load_scale_rows(w1_s, w1_scales)
        load_chunk(1)
        nc.sync.dma_start(
            w1_w[:].bitcast(I32).rearrange("p (a c) -> p a c", a=PASSES),
            w1_words.rearrange("a p c -> p a c").bitcast(I32),
        )
        load_chunk(2)
        idx3 = load_list("idx3", offs3)
        load_chunk(3)
        load_page(0)

        deal_gain()
        for a in range(PASSES):
            nc.vector.tensor_copy(v_w[a][:], tab_w[a][:].indirect(idx[:]))
            nc.vector.tensor_copy(v_s[a][:], tab_s[:, a, :].indirect(idx[:]))

        for n in range(3):
            quantise_chunk(n, rounded(n), "vector")
        quantise_chunk(3, rounded_on("rounded3", "tab_w0"), "vector")
        angles(0, [tile[:] for tile in feat])
        scaled_tile = tile_on("scaled_pass0", "tab_w0", [P, TILES, PASS], F32)
        scaled = [scaled_tile[:, c, :] for c in range(TILES)]
        cosine_part(0, scaled)
        sum_part(0, scaled)

        for n in (4, 5, 6):
            load_chunk(n)
        for s in (1, 2):
            load_page(s)
        load_chunk(7)
        for s in (3, 4):
            load_page(s)

        turn(0)
        turn(1)
        for n in (4, 5):
            quantise_chunk(n, rounded(n), "scalar")
        turned.append(tile_on("turned2", "rounded_slot2", [P, S], F32)[:])
        turned.append(own_tile("turned3", [P, S], F32)[:])
        turn(2)
        turn(3)
        for s in range(PACK - 1):
            place(s)

        sines = tile_on("sines", "late", [P, 2, PASS], F32)
        quantise_chunk(6, rounded(6), "scalar")
        angles(1, [sines[:, c % 2, :] for c in range(TILES)])
        quantise_chunk(7, rounded_on("rounded7", "late"), "scalar")
        halves = [tile_on("scaled_" + tag, tag, [P, 2, PASS], F32) for tag in ("early", "late")]
        scaled = [halves[c // 2][:, c % 2, :] for c in range(TILES)]
        cosine_part(1, scaled)
        sum_part(1, scaled)
        turned_late = tile_on("turned_late", "raw3", [P, PACK, S], F32)
        turned.extend([turned_late[:, t, :] for t in range(PACK)])
        for s in range(PACK, SLICES):
            turn(s)
        place(PACK - 1)

        for t in range(PACK):
            for u in range(2):
                nc.sync.dma_start(raw[u][:, t, :], page[t][:, BANK * u : BANK * (u + 1)])

        for s in (5, 6):
            load_page(s)
        idx2 = load_list("idx2", offs2)
        for a in range(PASSES):
            load_words(tab2_w[a], tab2_words[a])
        for quad in range(P // QUAD):
            nc.sync.dma_start(
                tab2_s[QUAD * quad : QUAD * quad + 4 * PASSES, :].bitcast(I32),
                tab2_scales[:, 4 * quad : 4 * quad + 4, :].bitcast(I32),
            )
        load_page(7)
        nc.sync.dma_start(tie_rows[:], tie.rearrange("(c p) j -> p c j", p=P))
        p1 = load_list("p1", pos1)
        p2 = load_list("p2", pos2)
        with nc.allow_non_contiguous_dma("one value of mark for each partition and row tile"):
            nc.sync.dma_start(mark_rows[:], mark.rearrange("(c p) -> p c", p=P))

        for u, (tag, engine) in enumerate((("late", "vector"), ("early", "scalar"))):
            dst = rounded_on("rounded_page%d" % u, tag)
            weave(engine, dst, raw[u][:])
            quantise_page(u, dst)

        woven = tile_on("woven", "feat3", [P, 2, PACK * BANK], BF16)
        for s in range(PACK, SLICES):
            place(s)
            if s == SLICES - 1:
                v2_s = tile_on("v2_s", "gain3", [P, S2], U8)
                nc.vector.tensor_copy(v2_s[:], tab2_s[:].indirect(idx2[:]))
                v2_w = [gather_candidates(0, "raw3")]
            for u in range(2):
                nc.scalar.copy(
                    woven[:, u, :].rearrange("p (n t) -> p n t", t=PACK)[:, :, s - PACK],
                    page[s][:, BANK * u : BANK * (u + 1)],
                )
        for u in range(2):
            quantise_page(2 + u, woven[:, u, :])
        v2_w.append(gather_candidates(1, "feat3"))

        score_banks = ((4, 7), (0, 1), (2, 5), (3, 6))
        for m in range(TILES):
            for u in range(2):
                bank = banks[score_banks[m][u]]
                for a in range(PASSES):
                    nc.tensor.matmul_mx(
                        out=bank[:],
                        lhsT=v2_w[m // 2][:, a, block(m % 2)].bitcast(FP8X4), lhsT_scale=v2_s[4 * a : P, block(m)],
                        rhs=page_w[2 * a + u][:].bitcast(FP8X4), rhs_scale=page_s[2 * a + u][:],
                        start=(a == 0), stop=(a == PASSES - 1),
                    )
                nc.scalar.copy(score[m][:, BANK * u : BANK * (u + 1)], bank[:])

        def combine(m):
            if m < SUMMED_ON_TENSOR:
                sum_bank, back_bank = banks[score_banks[m][0]], banks[score_banks[m][1]]
                for c in range(TILES):
                    for term, opens in ((first[m], True), (second[m], False)):
                        nc.tensor.matmul(
                            sum_bank[:, block(c)], term[:, block(c)], ident[:],
                            start=opens, stop=not opens, is_transpose=True,
                        )
                sum_turned = tile_on("sum_turned%d" % m, "feat%d" % m, [P, PAIRS], F32)
                nc.scalar.copy(sum_turned[:], sum_bank[:])
                for c in range(TILES):
                    nc.tensor.transpose(back_bank[:, block(c)], sum_turned[:, block(c)], ident[:])
                nc.scalar.copy(first[m][:], back_bank[:])
                nc.scalar.dma_start(out[block(m), :], first[m][:])
            else:
                nc.vector.scalar_tensor_tensor(
                    first[m][:], first[m][:], mark_rows[:, m : m + 1], second[m][:], ALU.mult, ALU.add
                )
                nc.sync.dma_start(out[block(m), :], first[m][:])

        for m in range(TILES):
            nc.vector.tensor_copy(first[m][:], score[m][:].indirect(p1[:]))
            if m < SUMMED_ON_TENSOR:
                nc.scalar.activation(first[m][:], first[m][:], ACT.Copy, scale=mark_rows[:, m : m + 1])
            if m > 0:
                combine(m - 1)
            nc.vector.tensor_tensor(second[m][:], score[m][:].indirect(p2[:]), tie_rows[:, m, :], ALU.mult)
        combine(TILES - 1)
